import numpy as np
import ml_dtypes


def mxq(x, axis, fmt="e4m3"):
    dtype, down = {"e4m3": (ml_dtypes.float8_e4m3fn, 7), "e5m2": (ml_dtypes.float8_e5m2, 14)}[fmt]
    v = np.moveaxis(np.asarray(x, np.float32).astype(ml_dtypes.bfloat16).astype(np.float64), axis, -1)
    blocks = v.reshape(v.shape[:-1] + (-1, 32))
    amax = np.abs(blocks).max(-1, keepdims=True)
    byte = np.maximum(np.where(amax > 0, np.frexp(amax)[1] - 1 + 127, 0) - down, 1)
    scale = np.exp2(byte - 127.0)
    codes = (blocks / scale).astype(np.float32).astype(dtype).astype(np.float64)
    return np.moveaxis((codes * scale).reshape(v.shape), -1, axis)


WIDE = False


def mx_kscale(k, group=512):
    if not WIDE:
        return np.ones(k)
    levels = np.array([18, -18])
    if group != 512:
        return np.exp2(np.random.permutation(np.resize(levels, k // group))).repeat(group)
    if k % 512:
        return np.exp2(np.random.permutation(np.resize(levels, k // 32))).repeat(32)
    a = np.empty((k // 512, 16))
    for p in range(k // 512):
        a[p, :8] = np.random.permutation(np.resize(levels, 8))
        for g in range(8):
            far = levels[np.abs(levels - a[p, g]) >= 10]
            a[p, g + 8] = far[np.random.randint(len(far))]
    return np.exp2(a.ravel()).repeat(32)


def f64(x):
    return np.asarray(x).astype(np.float64)


G, D, M, N = 8, 128, 128, 512


def setup_inputs():
    n = np.random.standard_normal
    s = mx_kscale(D, 0)[:, None]
    return {
        "x": (n((G, D, N)) * s).astype(np.float32),
        "w": (n((G, D, M)) / np.sqrt(D) / s).astype(np.float32),
    }


def reference(x, w):
    xq = mxq(f64(x), 1, "e4m3")
    y = mxq(f64(w), 1, "e4m3").transpose(0, 2, 1) @ xq
    y = 1.0 / (1.0 + np.exp(-(y)))
    return y

@@ -1,0 +1,100 @@
+from contextlib import ExitStack
+
+import concourse.mybir as mybir
+
+G, D, M, N = 8, 128, 128, 512
+FLOPS = 2 * G * D * M * N
+
+F32 = mybir.dt.float32
+BF16 = mybir.dt.bfloat16
+U32 = mybir.dt.uint32
+U8 = mybir.dt.uint8
+FP8X4 = mybir.dt.float8_e4m3fn_x4
+SIGMOID = mybir.ActivationFunctionType.Sigmoid
+
+P = 128
+PACK = 4
+ROWS = D // PACK
+SIDE = P // ROWS
+SETS = G // SIDE
+STRIP = 128
+CHUNK = 256
+LINE = 4
+
+
+def tile_rows_glin_sigmoid_kernel(tc, x, w, out):
+    nc = tc.nc
+    x_sets = x.rearrange("(s c) (p j) n -> s (c p) j n", c=SIDE, j=PACK)
+    w_sets = w.rearrange("(s c) (p j) m -> s (c p) j m", c=SIDE, j=PACK)
+    chunks = [(s, n0) for s in range(SETS) for n0 in range(0, N, CHUNK)]
+
+    with ExitStack() as ctx:
+        sb = ctx.enter_context(tc.tile_pool(name="sb", bufs=1))
+        ps = ctx.enter_context(tc.psum_pool(name="ps", bufs=1))
+        ctx.enter_context(tc.manual_schedule())
+
+        def load(name, src):
+            raw = sb.tile([P, PACK, src.shape[2]], F32, name=name)
+            nc.sync.dma_start(out=raw[:], in_=src)
+            return raw
+
+        def interleave(name, raw, n0):
+            grouped = sb.tile([P, STRIP, PACK], BF16, name=name, align_bytes=64)
+            nc.vector.tensor_copy(
+                out=grouped[:].rearrange("p (c i) j -> p c j i", i=LINE),
+                in_=raw[:, :, n0 : n0 + STRIP].rearrange("p j (c i) -> p c j i", i=LINE),
+            )
+            return grouped
+
+        def quantize(name, grouped):
+            codes = sb.tile([P, STRIP], U32, name=name + "c", align_bytes=64)
+            scales = sb.tile([P, STRIP], U8, name=name + "s", align_bytes=64)
+            nc.vector.quantize_mx(
+                out=codes[:].bitcast(FP8X4), scales=scales[:], in_=grouped[:].rearrange("p n j -> p (n j)")
+            )
+            return codes, scales
+
+        w_raw = {}
+        x_raw = {}
+        for i, (s, n0) in enumerate(chunks):
+            if n0 == 0:
+                w_raw[s] = load("w_raw%d" % s, w_sets[s])
+            x_raw[i] = load("x_raw%d" % i, x_sets[s][:, :, n0 : n0 + CHUNK])
+
+        banks = [[ps.tile([P, N], F32, name="bank%d_%d" % (b, c)) for c in range(SIDE)] for b in range(2)]
+        res0 = [sb.tile([P, N], F32, name="res0_%d" % c) for c in range(SIDE)]
+        w_q = {}
+        for i, (s, n0) in enumerate(chunks):
+            if n0 == 0:
+                wg = interleave("w_g%d" % s, w_raw[s], 0)
+                if s == 0:
+                    w_q[s] = quantize("w_q%d" % s, wg)
+            grouped = [interleave("x_g%d_%d" % (i, t), x_raw[i], t * STRIP) for t in range(CHUNK // STRIP)]
+            if s not in w_q:
+                w_q[s] = quantize("w_q%d" % s, wg)
+            wc, ws = w_q[s]
+            for t in range(CHUNK // STRIP):
+                xc, xs = quantize("x_q%d_%d" % (i, t), grouped[t])
+                for c in range(SIDE):
+                    rows = slice(c * ROWS, (c + 1) * ROWS)
+                    nc.tensor.matmul_mx(
+                        out=banks[i % 2][c][:, t * STRIP : (t + 1) * STRIP],
+                        lhsT=wc[rows, :].bitcast(FP8X4),
+                        lhsT_scale=ws[rows, :],
+                        rhs=xc[rows, :].bitcast(FP8X4),
+                        rhs_scale=xs[rows, :],
+                        start=True,
+                        stop=True,
+                    )
+            if s == 0:
+                for c in range(SIDE):
+                    nc.scalar.activation(out=res0[c][:, n0 : n0 + CHUNK], in_=banks[i % 2][c][:, 0:CHUNK], func=SIGMOID)
+                    if n0 + CHUNK == N:
+                        nc.sync.dma_start(out=out[c], in_=res0[c][:])
+            else:
+                for c0 in range(0, SIDE, 2):
+                    res = sb.tile([P, 2, CHUNK], F32, name="res%d_%d" % (i, c0))
+                    for c in range(c0, c0 + 2):
+                        nc.scalar.activation(out=res[:, c - c0, :], in_=banks[i % 2][c][:, 0:CHUNK], func=SIGMOID)
+                    g0 = s * SIDE + c0
+                    nc.sync.dma_start(out=out[g0 : g0 + 2, :, n0 : n0 + CHUNK].rearrange("g m n -> m g n"), in_=res[:])

@@ -62,7 +62,6 @@ def tile_rows_glin_sigmoid_kernel(tc, x, w, out):
             x_raw[i] = load("x_raw%d" % i, x_sets[s][:, :, n0 : n0 + CHUNK])
 
         banks = [[ps.tile([P, N], F32, name="bank%d_%d" % (b, c)) for c in range(SIDE)] for b in range(2)]
-        res0 = [sb.tile([P, N], F32, name="res0_%d" % c) for c in range(SIDE)]
         w_q = {}
         for i, (s, n0) in enumerate(chunks):
             if n0 == 0:
@@ -86,15 +85,9 @@ def tile_rows_glin_sigmoid_kernel(tc, x, w, out):
                         start=True,
                         stop=True,
                     )
-            if s == 0:
-                for c in range(SIDE):
-                    nc.scalar.activation(out=res0[c][:, n0 : n0 + CHUNK], in_=banks[i % 2][c][:, 0:CHUNK], func=SIGMOID)
-                    if n0 + CHUNK == N:
-                        nc.sync.dma_start(out=out[c], in_=res0[c][:])
-            else:
-                for c0 in range(0, SIDE, 2):
-                    res = sb.tile([P, 2, CHUNK], F32, name="res%d_%d" % (i, c0))
-                    for c in range(c0, c0 + 2):
-                        nc.scalar.activation(out=res[:, c - c0, :], in_=banks[i % 2][c][:, 0:CHUNK], func=SIGMOID)
-                    g0 = s * SIDE + c0
-                    nc.sync.dma_start(out=out[g0 : g0 + 2, :, n0 : n0 + CHUNK].rearrange("g m n -> m g n"), in_=res[:])
+            for c0 in range(0, SIDE, 2):
+                res = sb.tile([P, 2, CHUNK], F32, name="res%d_%d" % (i, c0))
+                for c in range(c0, c0 + 2):
+                    nc.scalar.activation(out=res[:, c - c0, :], in_=banks[i % 2][c][:, 0:CHUNK], func=SIGMOID)
+                g0 = s * SIDE + c0
+                nc.sync.dma_start(out=out[g0 : g0 + 2, :, n0 : n0 + CHUNK].rearrange("g m n -> m g n"), in_=res[:])

@@ -62,32 +62,31 @@ def tile_rows_glin_sigmoid_kernel(tc, x, w, out):
             x_raw[i] = load("x_raw%d" % i, x_sets[s][:, :, n0 : n0 + CHUNK])
 
         banks = [[ps.tile([P, N], F32, name="bank%d_%d" % (b, c)) for c in range(SIDE)] for b in range(2)]
-        w_q = {}
         for i, (s, n0) in enumerate(chunks):
             if n0 == 0:
-                wg = interleave("w_g%d" % s, w_raw[s], 0)
-                if s == 0:
-                    w_q[s] = quantize("w_q%d" % s, wg)
+                wc, ws = quantize("w_q%d" % s, interleave("w_g%d" % s, w_raw[s], 0))
             grouped = [interleave("x_g%d_%d" % (i, t), x_raw[i], t * STRIP) for t in range(CHUNK // STRIP)]
-            if s not in w_q:
-                w_q[s] = quantize("w_q%d" % s, wg)
-            wc, ws = w_q[s]
-            for t in range(CHUNK // STRIP):
-                xc, xs = quantize("x_q%d_%d" % (i, t), grouped[t])
-                for c in range(SIDE):
-                    rows = slice(c * ROWS, (c + 1) * ROWS)
-                    nc.tensor.matmul_mx(
-                        out=banks[i % 2][c][:, t * STRIP : (t + 1) * STRIP],
-                        lhsT=wc[rows, :].bitcast(FP8X4),
-                        lhsT_scale=ws[rows, :],
-                        rhs=xc[rows, :].bitcast(FP8X4),
-                        rhs_scale=xs[rows, :],
-                        start=True,
-                        stop=True,
-                    )
+            x_q = [quantize("x_q%d_%d" % (i, t), grouped[t]) for t in range(CHUNK // STRIP)]
             for c0 in range(0, SIDE, 2):
-                res = sb.tile([P, 2, CHUNK], F32, name="res%d_%d" % (i, c0))
-                for c in range(c0, c0 + 2):
+                for t in range(CHUNK // STRIP):
+                    xc, xs = x_q[t]
+                    for c in range(c0, c0 + 2):
+                        rows = slice(c * ROWS, (c + 1) * ROWS)
+                        nc.tensor.matmul_mx(
+                            out=banks[i % 2][c][:, t * STRIP : (t + 1) * STRIP],
+                            lhsT=wc[rows, :].bitcast(FP8X4),
+                            lhsT_scale=ws[rows, :],
+                            rhs=xc[rows, :].bitcast(FP8X4),
+                            rhs_scale=xs[rows, :],
+                            start=True,
+                            stop=True,
+                        )
+            spans = [(0, 2), (2, 3), (3, 4)] if i == len(chunks) - 1 else [(0, 2), (2, 4)]
+            for c0, c1 in spans:
+                res = sb.tile([P, c1 - c0, CHUNK], F32, name="res%d_%d" % (i, c0))
+                for c in range(c0, c1):
                     nc.scalar.activation(out=res[:, c - c0, :], in_=banks[i % 2][c][:, 0:CHUNK], func=SIGMOID)
-                g0 = s * SIDE + c0
-                nc.sync.dma_start(out=out[g0 : g0 + 2, :, n0 : n0 + CHUNK].rearrange("g m n -> m g n"), in_=res[:])
+                g0 = s * SIDE
+                nc.sync.dma_start(
+                    out=out[g0 + c0 : g0 + c1, :, n0 : n0 + CHUNK].rearrange("g m n -> m g n"), in_=res[:]
+                )

from contextlib import ExitStack

import concourse.mybir as mybir

G, D, M, N = 8, 128, 128, 512
FLOPS = 2 * G * D * M * N

F32 = mybir.dt.float32
BF16 = mybir.dt.bfloat16
U32 = mybir.dt.uint32
U8 = mybir.dt.uint8
FP8X4 = mybir.dt.float8_e4m3fn_x4
SIGMOID = mybir.ActivationFunctionType.Sigmoid

P = 128
PACK = 4
ROWS = D // PACK
SIDE = P // ROWS
SETS = G // SIDE
STRIP = 128
CHUNK = 256
LINE = 4


def tile_rows_glin_sigmoid_kernel(tc, x, w, out):
    nc = tc.nc
    x_sets = x.rearrange("(s c) (p j) n -> s (c p) j n", c=SIDE, j=PACK)
    w_sets = w.rearrange("(s c) (p j) m -> s (c p) j m", c=SIDE, j=PACK)
    chunks = [(s, n0) for s in range(SETS) for n0 in range(0, N, CHUNK)]

    with ExitStack() as ctx:
        sb = ctx.enter_context(tc.tile_pool(name="sb", bufs=1))
        ps = ctx.enter_context(tc.psum_pool(name="ps", bufs=1))
        ctx.enter_context(tc.manual_schedule())

        def load(name, src):
            raw = sb.tile([P, PACK, src.shape[2]], F32, name=name)
            nc.sync.dma_start(out=raw[:], in_=src)
            return raw

        def interleave(name, raw, n0):
            grouped = sb.tile([P, STRIP, PACK], BF16, name=name, align_bytes=64)
            nc.vector.tensor_copy(
                out=grouped[:].rearrange("p (c i) j -> p c j i", i=LINE),
                in_=raw[:, :, n0 : n0 + STRIP].rearrange("p j (c i) -> p c j i", i=LINE),
            )
            return grouped

        def quantize(name, grouped):
            codes = sb.tile([P, STRIP], U32, name=name + "c", align_bytes=64)
            scales = sb.tile([P, STRIP], U8, name=name + "s", align_bytes=64)
            nc.vector.quantize_mx(
                out=codes[:].bitcast(FP8X4), scales=scales[:], in_=grouped[:].rearrange("p n j -> p (n j)")
            )
            return codes, scales

        w_raw = {}
        x_raw = {}
        for i, (s, n0) in enumerate(chunks):
            if n0 == 0:
                w_raw[s] = load("w_raw%d" % s, w_sets[s])
            x_raw[i] = load("x_raw%d" % i, x_sets[s][:, :, n0 : n0 + CHUNK])

        banks = [[ps.tile([P, N], F32, name="bank%d_%d" % (b, c)) for c in range(SIDE)] for b in range(2)]
        for i, (s, n0) in enumerate(chunks):
            if n0 == 0:
                wc, ws = quantize("w_q%d" % s, interleave("w_g%d" % s, w_raw[s], 0))
            grouped = [interleave("x_g%d_%d" % (i, t), x_raw[i], t * STRIP) for t in range(CHUNK // STRIP)]
            x_q = [quantize("x_q%d_%d" % (i, t), grouped[t]) for t in range(CHUNK // STRIP)]
            for c0 in range(0, SIDE, 2):
                for t in range(CHUNK // STRIP):
                    xc, xs = x_q[t]
                    for c in range(c0, c0 + 2):
                        rows = slice(c * ROWS, (c + 1) * ROWS)
                        nc.tensor.matmul_mx(
                            out=banks[i % 2][c][:, t * STRIP : (t + 1) * STRIP],
                            lhsT=wc[rows, :].bitcast(FP8X4),
                            lhsT_scale=ws[rows, :],
                            rhs=xc[rows, :].bitcast(FP8X4),
                            rhs_scale=xs[rows, :],
                            start=True,
                            stop=True,
                        )
            spans = [(0, 2), (2, 3), (3, 4)] if i == len(chunks) - 1 else [(0, 2), (2, 4)]
            for c0, c1 in spans:
                res = sb.tile([P, c1 - c0, CHUNK], F32, name="res%d_%d" % (i, c0))
                for c in range(c0, c1):
                    nc.scalar.activation(out=res[:, c - c0, :], in_=banks[i % 2][c][:, 0:CHUNK], func=SIGMOID)
                g0 = s * SIDE
                nc.sync.dma_start(
                    out=out[g0 + c0 : g0 + c1, :, n0 : n0 + CHUNK].rearrange("g m n -> m g n"), in_=res[:]
                )
